import numpy as np, ml_dtypes
CORES = [35,38,43,46]
N = 4
import mx_ref
NC, HD, G = 128, 3, 4
C, DEC = np.float32(0.029), np.float32(0.9)
BF = ml_dtypes.bfloat16
def cut(t, i, w=512):
    return t[:, w * i:w * i + w]
def tile(rs):
    return np.stack(rs, axis=2).reshape(128, -1).astype(BF)
def layer(w, X):
    out = []
    for i in range(G):
        for t in range(len(X)):
            p = mx_ref.matmul(mx_ref.quantize(cut(w, len(X) * i + t)), X[t])
            z = p if t == 0 else z + p
        out.append(z)
    return out
def pick(b):
    s = np.zeros((128, 128, 4), np.float32)
    s[np.arange(128), np.arange(128), b] = 1.0
    return mx_ref.quantize(s.reshape(128, 512).astype(BF))
def setup_inputs(rng):
    def f(*shape):
        return mx_ref.flush((rng.standard_normal(shape, dtype=np.float32) * np.exp2(rng.integers(-2, 3, shape[:-1] + (1,)))).astype(BF))
    return {"k": f(N, 128, HD * 4 * 512), "v": f(N, 128, HD * 512), "q": f(N, 128, HD * 4 * NC)}
def setup_inputs_blocks(rng):
    d = setup_inputs(rng)
    for k in ("k", "v", "q"): d[k] = mx_ref.spread(d[k], rng, 4)
    return d
def setup_inputs_wide(rng):
    d = setup_inputs(rng)
    for k in ("k", "v", "q"): d[k] = mx_ref.flush((d[k].astype(np.float32) * np.exp2(rng.integers(-4, 5, (N, 1, 1))).astype(np.float32)).astype(BF))
    return d
def setup_inputs_zeros(rng):
    d = setup_inputs(rng); v = d["v"].reshape(N, 128, -1, 4).copy()
    v[np.broadcast_to((rng.random((N, 1, v.shape[2], 1)) < 0.33), v.shape)] = 0
    d["v"] = v.reshape(d["v"].shape)
    return d
def reference(k, v, q):
    S = [pick(t) for t in range(4)]
    y = np.zeros((N, 128, HD * NC), np.float32)
    for a in range(HD):
        for r in range(N):
            R = [z * C for z in layer(cut(k[r], a, 4 * 512), [mx_ref.quantize(cut(v[r], a))])]
            if r > 0: R = [R[t] + mx_ref.matmul(S[t], s) * DEC for t in range(4)]
            s = mx_ref.quantize(tile(R))
            y[r][:, NC * a:NC * a + NC] = mx_ref.matmul(s, mx_ref.quantize(cut(q[r], a, 4 * NC)))
    return {"y": y}

@@ -1,0 +1,173 @@
+import numpy as np
+from concourse.mybir import dt, AluOpType, ActivationFunctionType
+
+NH, NB, NC, W = 3, 4, 128, 512
+C = float(np.float32(0.029))
+DEC = float(np.float32(0.9))
+
+SCRATCH = {
+    "kb": ("sbuf", [128, NH * NB * W], "bfloat16"),
+    "vb": ("sbuf", [128, NH * W], "bfloat16"),
+    "qb": ("sbuf", [128, NH * W], "bfloat16"),
+    "kc": ("sbuf", [128, NH * NB * NC], "float8_e4m3fn_x4"),
+    "kp": ("sbuf", [128, NH * NB * NC], "uint8"),
+    "vc": ("sbuf", [128, NH * NC], "float8_e4m3fn_x4"),
+    "vp": ("sbuf", [128, NH * NC], "uint8"),
+    "qc": ("sbuf", [128, NH * NC], "float8_e4m3fn_x4"),
+    "qp": ("sbuf", [128, NH * NC], "uint8"),
+    "ones": ("sbuf", [128, W + NB], "bfloat16"),
+    "band": ("sbuf", [128, W + NB], "bfloat16"),
+    "pc": ("sbuf", [128, NB * NC], "float8_e4m3fn_x4"),
+    "pp": ("sbuf", [128, NB * NC], "uint8"),
+    "zc": ("sbuf", [128, NH * NB * NC], "float32"),
+    "dd": ("sbuf", [128, NH * NB * NC], "float32"),
+    "tb": ("sbuf", [128, NH * W], "bfloat16"),
+    "tc": ("sbuf", [128, NH * NC], "float8_e4m3fn_x4"),
+    "tp": ("sbuf", [128, NH * NC], "uint8"),
+    "lc": ("sbuf", [128, NH * NC], "float8_e4m3fn_x4"),
+    "lp": ("sbuf", [128, NH * NC], "uint8"),
+    "ys": ("sbuf", [128, NH * NC], "float32"),
+    "ps": ("psum", [128, 512 * 8], "float32"),
+}
+SEMAPHORES = ["ten", "vec", "act", "gps", "sent", "arr0", "arr1", "arr2",
+              "v0", "k0", "v1", "k1", "k2", "q", "st"]
+
+ORDER = [
+    ["Z0", "D0", "Z1", "D1", "Z2", "D2", "Q", "Y0", "Y1", "Y2"],
+    ["S", "Z0", "Z1", "D0", "Z2", "D1", "D2", "Q", "Y0", "Y1", "Y2"],
+    ["S", "Z0", "Z1", "Z2", "D0", "Q", "Y0", "D1", "Y1", "D2", "Y2"],
+    ["S", "Z0", "Z1", "Z2", "Q", "D0", "Y0", "D1", "Y1", "D2", "Y2"],
+]
+
+
+def engines(mask):
+    return bin(mask).count("1")
+
+
+def rank_program(g, core, T, topo):
+    rank = T.rank_of(core)
+    if rank is None:
+        return
+    last = len(T.cores) - 1
+    queues = {"ten": g.tensor, "vec": g.vector, "act": g.scalar, "gps": g, "syn": g.sync}
+    issued = {}
+    seen = {}
+    IDENT = ActivationFunctionType.Identity
+
+    def wait(queue, deps):
+        for sem, val in deps:
+            if seen.get((queue, sem), 0) < val:
+                queues[queue].wait_ge(T.sem[sem], val)
+                seen[(queue, sem)] = val
+
+    def run(queue, deps, call, sem=None, n=1):
+        wait(queue, deps)
+        sem = queue if sem is None else sem
+        call().then_inc(T.sem[sem], n)
+        issued[sem] = issued.get(sem, 0) + n
+        return (sem, issued[sem])
+
+    def load(queue, sem, out, in_):
+        return run(queue, [], lambda: queues[queue].dma_start(out, in_), sem, 16)
+
+    H = NB * W
+    v0 = load("act", "v0", T.vb[:, 0:W], T.v[:, 0:W])
+    kl = [load("syn", "k0", T.kb[:, 0:H], T.k[:, 0:H])]
+    v1 = load("act", "v1", T.vb[:, W:NH * W], T.v[:, W:NH * W])
+    for a in range(1, NH):
+        kl.append(load("syn", "k%d" % a, T.kb[:, a * H:(a + 1) * H], T.k[:, a * H:(a + 1) * H]))
+    ql = load("act", "q", T.qb[:], T.q[:])
+    vl = [v0, v1, v1]
+
+    reader = [None] * 8
+    turn = [0]
+
+    def mx(wc, wp, xc, xp, deps):
+        b = turn[0] % 8
+        turn[0] += 1
+        out = T.ps[:, 512 * b:512 * b + NC]
+        d = deps + ([reader[b]] if reader[b] else [])
+        return b, out, run("ten", d, lambda: g.tensor.matmul_mx(out, wc, wp, xc, xp, True, True))
+
+    def quant(codes, plane, j, src, deps):
+        return run("vec", deps, lambda: g.vector.quantize_mx(codes[:, NC * j:NC * (j + 1)], plane[:, NC * j:NC * (j + 1)], src))
+
+    def from_psum(bank, out, src, done, scale):
+        t = run("act", [done], lambda: g.scalar.activation(out, src, IDENT, scale=scale))
+        reader[bank] = t
+        return t
+
+    def col(t, j):
+        return t[:, NC * j:NC * (j + 1)]
+
+    def lane(a, b):
+        return T.tb[:, W * a + b:W * (a + 1):NB]
+
+    S, Z, Qt, made, arrive = {}, {}, {}, {}, {}
+
+    def do_S():
+        t = run("vec", [], lambda: g.vector.memset(T.ones[:], 1.0))
+        t = run("gps", [t], lambda: g.affine_select(T.band[:], T.ones[:], [[-1, W + NB]], AluOpType.is_equal, 0.0, NB - 1, NB))
+        for b in range(NB):
+            S[b] = quant(T.pc, T.pp, b, T.band[:, NB - 1 - b:NB - 1 - b + W], [t])
+
+    def do_Z(a):
+        tv = quant(T.vc, T.vp, a, T.vb[:, W * a:W * (a + 1)], [vl[a]])
+        for b in range(NB):
+            i = NB * a + b
+            tk = quant(T.kc, T.kp, i, T.kb[:, W * i:W * (i + 1)], [kl[a]])
+            bank, p, t = mx(col(T.kc, i), col(T.kp, i), col(T.vc, a), col(T.vp, a), [tv, tk])
+            Z[a, b] = from_psum(bank, lane(a, b) if rank == 0 else col(T.zc, i), p, t, C)
+
+    def do_D(a):
+        ready = []
+        for b in range(NB):
+            if rank == 0:
+                ready.append(Z[a, b])
+                continue
+            i = NB * a + b
+            bank, p, t = mx(col(T.pc, b), col(T.pp, b), col(T.lc, a), col(T.lp, a), [S[b], arrive[a]])
+            t = from_psum(bank, col(T.dd, i), p, t, DEC)
+            ready.append(run("vec", [Z[a, b], t], lambda: g.vector.tensor_tensor(lane(a, b), col(T.zc, i), col(T.dd, i), AluOpType.add)))
+        made[a] = quant(T.tc, T.tp, a, T.tb[:, W * a:W * (a + 1)], ready)
+        if rank < last:
+            send(a)
+
+    def send(a):
+        dst = T.cores[rank + 1]
+        rid, pid, _ = topo.addr(dst)
+        m = topo.mask(core, dst)
+        wait("gps", [made[a]])
+        g.remote_dma(col(T.lc, a).bitcast(dt.uint8), col(T.tc, a).bitcast(dt.uint8),
+                     T.sem["arr%d" % a], T.sem.sent, pid, rid, m)
+        g.remote_dma(col(T.lp, a), col(T.tp, a), T.sem["arr%d" % a], T.sem.sent, pid, rid, m)
+        issued["sent"] = issued.get("sent", 0) + 2 * engines(m)
+
+    def do_Q():
+        for a in range(NH):
+            Qt[a] = quant(T.qc, T.qp, a, T.qb[:, W * a:W * (a + 1)], [ql])
+
+    def do_Y(a):
+        bank, p, t = mx(col(T.tc, a), col(T.tp, a), col(T.qc, a), col(T.qp, a), [made[a], Qt[a]])
+        t = from_psum(bank, col(T.ys, a), p, t, 1.0)
+        run("syn", [t], lambda: g.sync.dma_start(T.y[:, NC * a:NC * (a + 1)], col(T.ys, a)), "st", 16)
+
+    if rank > 0:
+        n = 2 * engines(topo.mask(T.cores[rank - 1], core))
+        for a in range(NH):
+            issued["arr%d" % a] = n
+            arrive[a] = ("arr%d" % a, n)
+
+    steps = {"S": do_S, "Q": do_Q}
+    for s in ORDER[rank]:
+        if s in steps:
+            steps[s]()
+        else:
+            {"Z": do_Z, "D": do_D, "Y": do_Y}[s[0]](int(s[1]))
+
+    for sem in SEMAPHORES:
+        if issued.get(sem):
+            if sem == "sent":
+                wait("gps", [(sem, issued[sem])])
+            else:
+                wait("syn", [(sem, issued[sem])])

@@ -33,15 +33,17 @@ SEMAPHORES = ["ten", "vec", "act", "gps", "sent", "arr0", "arr1", "arr2",
               "v0", "k0", "v1", "k1", "k2", "q", "st"]
 
 ORDER = [
-    ["Z0", "D0", "Z1", "D1", "Z2", "D2", "Q", "Y0", "Y1", "Y2"],
-    ["S", "Z0", "Z1", "D0", "Z2", "D1", "D2", "Q", "Y0", "Y1", "Y2"],
-    ["S", "Z0", "Z1", "Z2", "D0", "Q", "Y0", "D1", "Y1", "D2", "Y2"],
-    ["S", "Z0", "Z1", "Z2", "Q", "D0", "Y0", "D1", "Y1", "D2", "Y2"],
+    "Z0 D0 Z1 D1 Z2 D2 Q Y0 Y1 Y2".split(),
+    "S Z0 Z1 Z2 D0 D1 D2 Q Y0 Y1 Y2".split(),
+    "S Z0 Z1 Z2 D0 D1 D2 Q Y0 Y1 Y2".split(),
+    "S Z0 Z1 Z2 Q D0 D1 D2 Y0 Y1 Y2".split(),
 ]
+ENGINES = 8
 
 
-def engines(mask):
-    return bin(mask).count("1")
+def spread(mask, n):
+    e = [i for i in range(mask.bit_length()) if mask >> i & 1]
+    return sum(1 << i for i in e[::len(e) // n])
 
 
 def rank_program(g, core, T, topo):
@@ -76,7 +78,7 @@ def rank_program(g, core, T, topo):
     v1 = load("act", "v1", T.vb[:, W:NH * W], T.v[:, W:NH * W])
     for a in range(1, NH):
         kl.append(load("syn", "k%d" % a, T.kb[:, a * H:(a + 1) * H], T.k[:, a * H:(a + 1) * H]))
-    ql = load("act", "q", T.qb[:], T.q[:])
+    ql = load("syn", "q", T.qb[:], T.q[:])
     vl = [v0, v1, v1]
 
     reader = [None] * 8
@@ -136,12 +138,12 @@ def rank_program(g, core, T, topo):
     def send(a):
         dst = T.cores[rank + 1]
         rid, pid, _ = topo.addr(dst)
-        m = topo.mask(core, dst)
+        m = spread(topo.mask(core, dst), ENGINES)
         wait("gps", [made[a]])
         g.remote_dma(col(T.lc, a).bitcast(dt.uint8), col(T.tc, a).bitcast(dt.uint8),
                      T.sem["arr%d" % a], T.sem.sent, pid, rid, m)
         g.remote_dma(col(T.lp, a), col(T.tp, a), T.sem["arr%d" % a], T.sem.sent, pid, rid, m)
-        issued["sent"] = issued.get("sent", 0) + 2 * engines(m)
+        issued["sent"] = issued.get("sent", 0) + 2 * ENGINES
 
     def do_Q():
         for a in range(NH):
@@ -153,10 +155,9 @@ def rank_program(g, core, T, topo):
         run("syn", [t], lambda: g.sync.dma_start(T.y[:, NC * a:NC * (a + 1)], col(T.ys, a)), "st", 16)
 
     if rank > 0:
-        n = 2 * engines(topo.mask(T.cores[rank - 1], core))
         for a in range(NH):
-            issued["arr%d" % a] = n
-            arrive[a] = ("arr%d" % a, n)
+            issued["arr%d" % a] = 2 * ENGINES
+            arrive[a] = ("arr%d" % a, 2 * ENGINES)
 
     steps = {"S": do_S, "Q": do_Q}
     for s in ORDER[rank]:

import numpy as np
from concourse.mybir import dt, AluOpType, ActivationFunctionType

NH, NB, NC, W = 3, 4, 128, 512
C = float(np.float32(0.029))
DEC = float(np.float32(0.9))

SCRATCH = {
    "kb": ("sbuf", [128, NH * NB * W], "bfloat16"),
    "vb": ("sbuf", [128, NH * W], "bfloat16"),
    "qb": ("sbuf", [128, NH * W], "bfloat16"),
    "kc": ("sbuf", [128, NH * NB * NC], "float8_e4m3fn_x4"),
    "kp": ("sbuf", [128, NH * NB * NC], "uint8"),
    "vc": ("sbuf", [128, NH * NC], "float8_e4m3fn_x4"),
    "vp": ("sbuf", [128, NH * NC], "uint8"),
    "qc": ("sbuf", [128, NH * NC], "float8_e4m3fn_x4"),
    "qp": ("sbuf", [128, NH * NC], "uint8"),
    "ones": ("sbuf", [128, W + NB], "bfloat16"),
    "band": ("sbuf", [128, W + NB], "bfloat16"),
    "pc": ("sbuf", [128, NB * NC], "float8_e4m3fn_x4"),
    "pp": ("sbuf", [128, NB * NC], "uint8"),
    "zc": ("sbuf", [128, NH * NB * NC], "float32"),
    "dd": ("sbuf", [128, NH * NB * NC], "float32"),
    "tb": ("sbuf", [128, NH * W], "bfloat16"),
    "tc": ("sbuf", [128, NH * NC], "float8_e4m3fn_x4"),
    "tp": ("sbuf", [128, NH * NC], "uint8"),
    "lc": ("sbuf", [128, NH * NC], "float8_e4m3fn_x4"),
    "lp": ("sbuf", [128, NH * NC], "uint8"),
    "ys": ("sbuf", [128, NH * NC], "float32"),
    "ps": ("psum", [128, 512 * 8], "float32"),
}
SEMAPHORES = ["ten", "vec", "act", "gps", "sent", "arr0", "arr1", "arr2",
              "v0", "k0", "v1", "k1", "k2", "q", "st"]

ORDER = [
    "Z0 D0 Z1 D1 Z2 D2 Q Y0 Y1 Y2".split(),
    "S Z0 Z1 Z2 D0 D1 D2 Q Y0 Y1 Y2".split(),
    "S Z0 Z1 Z2 D0 D1 D2 Q Y0 Y1 Y2".split(),
    "S Z0 Z1 Z2 Q D0 D1 D2 Y0 Y1 Y2".split(),
]
ENGINES = 8


def spread(mask, n):
    e = [i for i in range(mask.bit_length()) if mask >> i & 1]
    return sum(1 << i for i in e[::len(e) // n])


def rank_program(g, core, T, topo):
    rank = T.rank_of(core)
    if rank is None:
        return
    last = len(T.cores) - 1
    queues = {"ten": g.tensor, "vec": g.vector, "act": g.scalar, "gps": g, "syn": g.sync}
    issued = {}
    seen = {}
    IDENT = ActivationFunctionType.Identity

    def wait(queue, deps):
        for sem, val in deps:
            if seen.get((queue, sem), 0) < val:
                queues[queue].wait_ge(T.sem[sem], val)
                seen[(queue, sem)] = val

    def run(queue, deps, call, sem=None, n=1):
        wait(queue, deps)
        sem = queue if sem is None else sem
        call().then_inc(T.sem[sem], n)
        issued[sem] = issued.get(sem, 0) + n
        return (sem, issued[sem])

    def load(queue, sem, out, in_):
        return run(queue, [], lambda: queues[queue].dma_start(out, in_), sem, 16)

    H = NB * W
    v0 = load("act", "v0", T.vb[:, 0:W], T.v[:, 0:W])
    kl = [load("syn", "k0", T.kb[:, 0:H], T.k[:, 0:H])]
    v1 = load("act", "v1", T.vb[:, W:NH * W], T.v[:, W:NH * W])
    for a in range(1, NH):
        kl.append(load("syn", "k%d" % a, T.kb[:, a * H:(a + 1) * H], T.k[:, a * H:(a + 1) * H]))
    ql = load("syn", "q", T.qb[:], T.q[:])
    vl = [v0, v1, v1]

    reader = [None] * 8
    turn = [0]

    def mx(wc, wp, xc, xp, deps):
        b = turn[0] % 8
        turn[0] += 1
        out = T.ps[:, 512 * b:512 * b + NC]
        d = deps + ([reader[b]] if reader[b] else [])
        return b, out, run("ten", d, lambda: g.tensor.matmul_mx(out, wc, wp, xc, xp, True, True))

    def quant(codes, plane, j, src, deps):
        return run("vec", deps, lambda: g.vector.quantize_mx(codes[:, NC * j:NC * (j + 1)], plane[:, NC * j:NC * (j + 1)], src))

    def from_psum(bank, out, src, done, scale):
        t = run("act", [done], lambda: g.scalar.activation(out, src, IDENT, scale=scale))
        reader[bank] = t
        return t

    def col(t, j):
        return t[:, NC * j:NC * (j + 1)]

    def lane(a, b):
        return T.tb[:, W * a + b:W * (a + 1):NB]

    S, Z, Qt, made, arrive = {}, {}, {}, {}, {}

    def do_S():
        t = run("vec", [], lambda: g.vector.memset(T.ones[:], 1.0))
        t = run("gps", [t], lambda: g.affine_select(T.band[:], T.ones[:], [[-1, W + NB]], AluOpType.is_equal, 0.0, NB - 1, NB))
        for b in range(NB):
            S[b] = quant(T.pc, T.pp, b, T.band[:, NB - 1 - b:NB - 1 - b + W], [t])

    def do_Z(a):
        tv = quant(T.vc, T.vp, a, T.vb[:, W * a:W * (a + 1)], [vl[a]])
        for b in range(NB):
            i = NB * a + b
            tk = quant(T.kc, T.kp, i, T.kb[:, W * i:W * (i + 1)], [kl[a]])
            bank, p, t = mx(col(T.kc, i), col(T.kp, i), col(T.vc, a), col(T.vp, a), [tv, tk])
            Z[a, b] = from_psum(bank, lane(a, b) if rank == 0 else col(T.zc, i), p, t, C)

    def do_D(a):
        ready = []
        for b in range(NB):
            if rank == 0:
                ready.append(Z[a, b])
                continue
            i = NB * a + b
            bank, p, t = mx(col(T.pc, b), col(T.pp, b), col(T.lc, a), col(T.lp, a), [S[b], arrive[a]])
            t = from_psum(bank, col(T.dd, i), p, t, DEC)
            ready.append(run("vec", [Z[a, b], t], lambda: g.vector.tensor_tensor(lane(a, b), col(T.zc, i), col(T.dd, i), AluOpType.add)))
        made[a] = quant(T.tc, T.tp, a, T.tb[:, W * a:W * (a + 1)], ready)
        if rank < last:
            send(a)

    def send(a):
        dst = T.cores[rank + 1]
        rid, pid, _ = topo.addr(dst)
        m = spread(topo.mask(core, dst), ENGINES)
        wait("gps", [made[a]])
        g.remote_dma(col(T.lc, a).bitcast(dt.uint8), col(T.tc, a).bitcast(dt.uint8),
                     T.sem["arr%d" % a], T.sem.sent, pid, rid, m)
        g.remote_dma(col(T.lp, a), col(T.tp, a), T.sem["arr%d" % a], T.sem.sent, pid, rid, m)
        issued["sent"] = issued.get("sent", 0) + 2 * ENGINES

    def do_Q():
        for a in range(NH):
            Qt[a] = quant(T.qc, T.qp, a, T.qb[:, W * a:W * (a + 1)], [ql])

    def do_Y(a):
        bank, p, t = mx(col(T.tc, a), col(T.tp, a), col(T.qc, a), col(T.qp, a), [made[a], Qt[a]])
        t = from_psum(bank, col(T.ys, a), p, t, 1.0)
        run("syn", [t], lambda: g.sync.dma_start(T.y[:, NC * a:NC * (a + 1)], col(T.ys, a)), "st", 16)

    if rank > 0:
        for a in range(NH):
            issued["arr%d" % a] = 2 * ENGINES
            arrive[a] = ("arr%d" % a, 2 * ENGINES)

    steps = {"S": do_S, "Q": do_Q}
    for s in ORDER[rank]:
        if s in steps:
            steps[s]()
        else:
            {"Z": do_Z, "D": do_D, "Y": do_Y}[s[0]](int(s[1]))

    for sem in SEMAPHORES:
        if issued.get(sem):
            if sem == "sent":
                wait("gps", [(sem, issued[sem])])
            else:
                wait("syn", [(sem, issued[sem])])
